import numpy as np
import ml_dtypes


def mxq(x, axis, fmt="e4m3"):
    dtype, down = {"e4m3": (ml_dtypes.float8_e4m3fn, 7), "e5m2": (ml_dtypes.float8_e5m2, 14)}[fmt]
    v = np.moveaxis(np.asarray(x, np.float32).astype(ml_dtypes.bfloat16).astype(np.float64), axis, -1)
    blocks = v.reshape(v.shape[:-1] + (-1, 32))
    amax = np.abs(blocks).max(-1, keepdims=True)
    byte = np.maximum(np.where(amax > 0, np.frexp(amax)[1] - 1 + 127, 0) - down, 1)
    scale = np.exp2(byte - 127.0)
    codes = (blocks / scale).astype(np.float32).astype(dtype).astype(np.float64)
    return np.moveaxis((codes * scale).reshape(v.shape), -1, axis)


WIDE = False


def mx_kscale(k):
    if not WIDE:
        return np.ones(k)
    levels = np.array([10, -10, 5, -5, 0])
    if k % 512:
        return np.exp2(np.random.permutation(np.resize(levels, k // 32))).repeat(32)
    a = np.empty((k // 512, 16))
    for p in range(k // 512):
        a[p, :8] = np.random.permutation(np.resize(levels, 8))
        for g in range(8):
            far = levels[np.abs(levels - a[p, g]) >= 10]
            a[p, g + 8] = far[np.random.randint(len(far))]
    return np.exp2(a.ravel()).repeat(32)


def f64(x):
    return np.asarray(x).astype(np.float64)


def striped(idx):
    return np.tile(np.asarray(idx).reshape(-1, 16).T, (8, 1)).astype(np.uint16)


def unstriped(offs):
    return offs[:16].T.reshape(-1).astype(np.int64)


E2M1 = np.array([0.0, 0.5, 1.0, 1.5, 2.0, 3.0, 4.0, 6.0, -0.0, -0.5, -1.0, -1.5, -2.0, -3.0, -4.0, -6.0])


def pack_weight(w, fmt):
    k, n = w.shape
    w = f64(np.asarray(w, np.float32).astype(ml_dtypes.bfloat16)).reshape(k // 32, 32, n)
    amax = np.abs(w).max(1)
    if fmt == "e4m3":
        byte = np.frexp(amax)[1] - 1 + 127 - 7
    else:
        mant, ex = np.frexp(amax / 6.0)
        byte = np.where(mant > 0.5, ex, ex - 1) + 127
    byte = np.clip(np.where(amax > 0, byte, 1), 1, 254)
    scaled = (w * np.exp2(127.0 - byte)[:, None, :]).reshape(k, n).astype(np.float32)
    by_word = np.ascontiguousarray(scaled.reshape(k // 512, 128, 4, n).transpose(0, 1, 3, 2))
    if fmt == "e4m3":
        words = by_word.astype(ml_dtypes.float8_e4m3fn).view(np.uint8)
    else:
        c = by_word.astype(ml_dtypes.float4_e2m1fn).view(np.uint8) & 0xF
        words = (c[..., 0::2] | (c[..., 1::2] << 4)).reshape(k // 512, 128, 2 * n)
    return np.ascontiguousarray(words), np.ascontiguousarray(byte.astype(np.uint8).reshape(k // 512, 16, n))


def unpack_weight(words, scales, fmt):
    g, _, n = scales.shape
    words = np.ascontiguousarray(words).reshape(g, 128, n, -1)
    if fmt == "e4m3":
        vals = words.view(ml_dtypes.float8_e4m3fn).astype(np.float64)
    else:
        nib = np.empty((g, 128, n, 4), np.uint8)
        nib[..., 0::2] = words & 0xF
        nib[..., 1::2] = words >> 4
        vals = E2M1[nib]
    vals = vals * np.repeat(np.exp2(scales.astype(np.float64) - 127.0), 8, axis=1)[..., None]
    return vals.transpose(0, 1, 3, 2).reshape(g * 512, n)


def sigmoid(v):
    return 1.0 / (1.0 + np.exp(-v))


D, K, U, I, E = 512, 512, 1024, 512, 256


def setup_inputs():
    n = np.random.standard_normal
    idx = np.random.permutation(U)[:I]
    idx2 = np.random.permutation(U)[:I]
    idx3 = np.random.permutation(U)[:I]
    fd = mx_kscale(D)
    fk = mx_kscale(K)
    notesp = pack_weight(n((D, U)) / fd[:, None], "e4m3")
    wbp = pack_weight(n((D, K)) * 1.0 / np.sqrt(D) * fd[:, None], "e2m1")
    wop = pack_weight(n((K, E)) * 1.0 / np.sqrt(K) / fk[:, None], "e4m3")
    return {
        "notes_words": notesp[0],
        "notes_scales": notesp[1],
        "wb_words": wbp[0],
        "wb_scales": wbp[1],
        "bias": (np.random.uniform(-0.6, 0.6, (K, 1))).astype(np.float32),
        "slope": (np.random.uniform(0.8, 2.0, (K, 1))).astype(np.float32),
        "kf": (np.random.uniform(0.5, 2.0, (K, 1)) * fk[:, None]).astype(np.float32),
        "wo_words": wop[0],
        "wo_scales": wop[1],
        "offs": striped(idx),
        "offs2": striped(idx2),
        "offs3": striped(idx3),
    }


def reference(notes_words, notes_scales, wb_words, wb_scales, bias, slope, kf, wo_words, wo_scales, offs, offs2, offs3):
    idx = unstriped(offs)
    idx2 = unstriped(offs2)
    idx3 = unstriped(offs3)
    notesu = unpack_weight(notes_words, notes_scales, "e4m3")
    wbu = unpack_weight(wb_words, wb_scales, "e2m1")
    wou = unpack_weight(wo_words, wo_scales, "e4m3")
    h1 = wbu.T @ notesu
    s1 = sigmoid(h1[:, idx] * f64(slope) + f64(bias))
    f1 = np.zeros((K, U))
    f1[:, idx2] = s1
    c1 = h1 + f1 * 2.0
    w = c1[:, idx3] * f64(kf)
    wq = mxq(w, 0, "e4m3")
    y = wou.T @ wq
    return y

@@ -1,0 +1,178 @@
+from contextlib import ExitStack
+
+import concourse.mybir as mybir
+
+D, K, U, I, E = 512, 512, 1024, 512, 256
+FLOPS = 2 * D * K * U + 2 * K * E * I
+
+F32 = mybir.dt.float32
+BF16 = mybir.dt.bfloat16
+I32 = mybir.dt.int32
+U32 = mybir.dt.uint32
+U16 = mybir.dt.uint16
+U8 = mybir.dt.uint8
+FP8X4 = mybir.dt.float8_e4m3fn_x4
+FP4X4 = mybir.dt.float4_e2m1fn_x4
+ALU = mybir.AluOpType
+ACT = mybir.ActivationFunctionType
+
+P = 128
+PACK = 4
+BANK = 512
+HALF = I // 2
+COLS = HALF // 16
+
+
+def tile_attend_gatehop_kernel(tc, notes_words, notes_scales, wb_words, wb_scales, bias, slope, kf,
+                                wo_words, wo_scales, offs, offs2, offs3, out):
+    nc = tc.nc
+    with ExitStack() as ctx:
+        sb = ctx.enter_context(tc.tile_pool(name="sb", bufs=1))
+        ps = ctx.enter_context(tc.psum_pool(name="ps", bufs=1))
+
+        def load_scale_rows(plane, rows, quadrants):
+            for q in quadrants:
+                nc.sync.dma_start(out=plane[32 * q : 32 * q + 4, :].bitcast(I32), in_=rows[0, 4 * q : 4 * q + 4, :].bitcast(I32))
+
+        wb_plane_raw = sb.tile([P, K], U8, name="wb_plane_raw", tag="raw_plane_then_f2", align_bytes=64)
+        notes_plane = sb.tile([P, U], U8, name="notes_plane", align_bytes=64)
+        wo_plane = sb.tile([P, E], U8, name="wo_plane", align_bytes=64)
+        nc.gpsimd.memset(wb_plane_raw[:].bitcast(U32), 0)
+
+        wb_raw = sb.tile([P, 2 * K], U8, name="wb_raw", tag="raw_words_then_f3", align_bytes=64)
+        load_scale_rows(wb_plane_raw, wb_scales, range(4))
+        nc.sync.dma_start(out=wb_raw[:].bitcast(I32), in_=wb_words[0].bitcast(I32))
+        load_scale_rows(notes_plane, notes_scales, range(2))
+        notes = sb.tile([P, U], U32, name="notes", align_bytes=64)
+        nc.sync.dma_start(out=notes[:].bitcast(I32), in_=notes_words[0].rearrange("p n t -> p (n t)").bitcast(I32))
+        load_scale_rows(notes_plane, notes_scales, range(2, 4))
+
+        list1 = sb.tile([P, I // 16], U16, name="list1")
+        list2 = sb.tile([P, I // 16], U16, name="list2")
+        list3 = sb.tile([P, I // 16], U16, name="list3")
+        slope4 = sb.tile([P, PACK], F32, name="slope4")
+        bias4 = sb.tile([P, PACK], F32, name="bias4")
+        kf4 = sb.tile([P, PACK], F32, name="kf4")
+        nc.sync.dma_start(list1[:], offs)
+        nc.sync.dma_start(out=slope4[:], in_=slope.rearrange("(p t) o -> p (t o)", t=PACK))
+        nc.sync.dma_start(out=bias4[:], in_=bias.rearrange("(p t) o -> p (t o)", t=PACK))
+        nc.sync.dma_start(list2[:], offs2)
+        nc.sync.dma_start(list3[:], offs3)
+        nc.sync.dma_start(out=kf4[:], in_=kf.rearrange("(p t) o -> p (t o)", t=PACK))
+        wo = sb.tile([P, E], U32, name="wo", align_bytes=64)
+        nc.sync.dma_start(out=wo[:].bitcast(I32), in_=wo_words[0].rearrange("p n t -> p (n t)").bitcast(I32))
+        load_scale_rows(wo_plane, wo_scales, range(4))
+
+        f = [sb.tile([P, U], F32, name="f%d" % t) for t in range(2)]
+        for t in range(2):
+            nc.vector.memset(f[t][:], 0.0)
+
+        wb = sb.tile([P, 2 * K], U8, name="wb", align_bytes=64)
+        wb_plane = sb.tile([P, K], U8, name="wb_plane", align_bytes=64)
+        nc.scalar.copy(out=wb[:].bitcast(U16).rearrange("p (t m) -> p t m", t=PACK),
+                       in_=wb_raw[:].bitcast(U16).rearrange("p (m t) -> p t m", t=PACK))
+        nc.vector.tensor_copy(out=wb_plane[:].rearrange("p (t m) -> p t m", t=PACK),
+                              in_=wb_plane_raw[:].rearrange("p (m t) -> p t m", t=PACK))
+        f.append(sb.tile([P, U], F32, name="f2", tag="raw_plane_then_f2", align_bytes=64))
+        f.append(sb.tile([P, U], F32, name="f3", tag="raw_words_then_f3", align_bytes=64))
+        nc.gpsimd.memset(f[3][:], 0.0)
+        nc.gpsimd.memset(f[2][:], 0.0)
+
+        banks = [[ps.tile([P, BANK], F32, name="h_ps%d_%d" % (t, b), tag="bank%d" % (2 * t + b)) for b in range(2)] for t in range(PACK)]
+        for t in range(PACK):
+            for b in range(2):
+                nc.tensor.matmul_mx(
+                    out=banks[t][b][:],
+                    lhsT=wb[:, 2 * P * t : 2 * P * (t + 1)].bitcast(FP4X4),
+                    lhsT_scale=wb_plane[:, P * t : P * (t + 1)],
+                    rhs=notes[:, BANK * b : BANK * (b + 1)].bitcast(FP8X4),
+                    rhs_scale=notes_plane[:, BANK * b : BANK * (b + 1)],
+                    start=True, stop=True)
+
+        h = [sb.tile([P, U], F32, name="h%d" % t) for t in range(PACK)]
+        s = [sb.tile([P, I], F32, name="s%d" % t) for t in range(PACK)]
+        c = [sb.tile([P, U], F32, name="c%d" % t) for t in range(PACK)]
+        g = [sb.tile([P, PACK, HALF], F32, name="g%d" % a) for a in range(2)]
+
+        def copy_v(t, b):
+            nc.vector.tensor_copy(out=h[t][:, BANK * b : BANK * (b + 1)], in_=banks[t][b][:])
+
+        def copy_s(t, b):
+            nc.scalar.copy(out=h[t][:, BANK * b : BANK * (b + 1)], in_=banks[t][b][:])
+
+        def sigmoid(t):
+            nc.scalar.activation(out=s[t][:], in_=h[t][:].indirect(list1[:]), func=ACT.Sigmoid,
+                                 bias=bias4[:, t : t + 1], scale=slope4[:, t : t + 1])
+
+        def scatter_v(t):
+            nc.vector.tensor_copy(out=f[t][:].indirect(list2[:]), in_=s[t][:])
+
+        def scatter_s(t):
+            for a in range(2):
+                nc.scalar.activation(out=f[t][:].indirect(list2[:, COLS * a : COLS * (a + 1)]),
+                                     in_=s[t][:, HALF * a : HALF * (a + 1)], func=ACT.Copy)
+
+        def add(t):
+            for b in range(2):
+                cols = slice(BANK * b, BANK * (b + 1))
+                nc.vector.scalar_tensor_tensor(out=c[t][:, cols], in0=f[t][:, cols], scalar=2.0, in1=banks[t][b][:],
+                                               op0=ALU.mult, op1=ALU.add)
+
+        def gather_v(t, a):
+            nc.vector.tensor_copy(out=g[a][:, t, :], in_=c[t][:].indirect(list3[:, COLS * a : COLS * (a + 1)]))
+
+        def gather_s(t, a):
+            nc.scalar.activation(out=g[a][:, t, :], in_=c[t][:].indirect(list3[:, COLS * a : COLS * (a + 1)]), func=ACT.Copy)
+
+        copy_v(0, 0)
+        copy_s(0, 1)
+        sigmoid(0)
+        copy_v(1, 0)
+        copy_v(1, 1)
+        sigmoid(1)
+        copy_v(2, 0)
+        copy_v(2, 1)
+        scatter_v(0)
+        sigmoid(2)
+        copy_s(3, 0)
+        copy_s(3, 1)
+        sigmoid(3)
+        scatter_s(2)
+        scatter_v(1)
+        scatter_s(3)
+        add(0)
+        add(1)
+        add(2)
+        gather_v(0, 0)
+        gather_v(0, 1)
+        add(3)
+        gather_s(1, 0)
+        gather_s(2, 0)
+        gather_v(3, 0)
+        gather_s(1, 1)
+        gather_s(2, 1)
+        gather_s(3, 1)
+
+        kf_view = kf4[:].unsqueeze(1).unsqueeze(3).to_broadcast([P, HALF // 4, PACK, 4])
+        for a in range(2):
+            w = sb.tile([P, HALF, PACK], BF16, name="w%d" % a, align_bytes=64)
+            nc.vector.tensor_tensor(out=w[:].rearrange("p (c i) t -> p c t i", i=4),
+                                    in0=g[a][:].rearrange("p t (c i) -> p c t i", i=4), in1=kf_view, op=ALU.mult)
+            wq = sb.tile([P, HALF], U32, name="wq%d" % a, align_bytes=64)
+            wq_plane = sb.tile([P, HALF], U8, name="wq_plane%d" % a, align_bytes=64)
+            nc.vector.quantize_mx(out=wq[:].bitcast(FP8X4), scales=wq_plane[:], in_=w[:].rearrange("p i t -> p (i t)"))
+            for e in range(2):
+                y_ps = ps.tile([P, HALF], F32, name="y_ps%d_%d" % (a, e), tag="bank%d" % (2 * a + e))
+                nc.tensor.matmul_mx(
+                    out=y_ps[:],
+                    lhsT=wo[:, P * e : P * (e + 1)].bitcast(FP8X4),
+                    lhsT_scale=wo_plane[:, P * e : P * (e + 1)],
+                    rhs=wq[:].bitcast(FP8X4),
+                    rhs_scale=wq_plane[:],
+                    start=True, stop=True)
+                y = sb.tile([P, HALF], F32, name="y%d_%d" % (a, e))
+                if a == 1 and e == 1:
+                    nc.vector.tensor_copy(out=y[:], in_=y_ps[:])
+                else:
+                    nc.scalar.copy(out=y[:], in_=y_ps[:])
+                nc.sync.dma_start(out=out[P * e : P * (e + 1), HALF * a : HALF * (a + 1)], in_=y[:])

@@ -21,6 +21,7 @@ PACK = 4
 BANK = 512
 HALF = I // 2
 COLS = HALF // 16
+CHUNKS = [(0, 256), (256, 128), (384, 128)]
 
 
 def tile_attend_gatehop_kernel(tc, notes_words, notes_scales, wb_words, wb_scales, bias, slope, kf,
@@ -40,9 +41,9 @@ def tile_attend_gatehop_kernel(tc, notes_words, notes_scales, wb_words, wb_scale
         nc.gpsimd.memset(wb_plane_raw[:].bitcast(U32), 0)
 
         wb_raw = sb.tile([P, 2 * K], U8, name="wb_raw", tag="raw_words_then_f3", align_bytes=64)
+        load_scale_rows(notes_plane, notes_scales, range(2))
         load_scale_rows(wb_plane_raw, wb_scales, range(4))
         nc.sync.dma_start(out=wb_raw[:].bitcast(I32), in_=wb_words[0].bitcast(I32))
-        load_scale_rows(notes_plane, notes_scales, range(2))
         notes = sb.tile([P, U], U32, name="notes", align_bytes=64)
         nc.sync.dma_start(out=notes[:].bitcast(I32), in_=notes_words[0].rearrange("p n t -> p (n t)").bitcast(I32))
         load_scale_rows(notes_plane, notes_scales, range(2, 4))
@@ -69,7 +70,7 @@ def tile_attend_gatehop_kernel(tc, notes_words, notes_scales, wb_words, wb_scale
 
         wb = sb.tile([P, 2 * K], U8, name="wb", align_bytes=64)
         wb_plane = sb.tile([P, K], U8, name="wb_plane", align_bytes=64)
-        nc.scalar.copy(out=wb[:].bitcast(U16).rearrange("p (t m) -> p t m", t=PACK),
+        nc.vector.tensor_copy(out=wb[:].bitcast(U16).rearrange("p (t m) -> p t m", t=PACK),
                        in_=wb_raw[:].bitcast(U16).rearrange("p (m t) -> p t m", t=PACK))
         nc.vector.tensor_copy(out=wb_plane[:].rearrange("p (t m) -> p t m", t=PACK),
                               in_=wb_plane_raw[:].rearrange("p (m t) -> p t m", t=PACK))
@@ -90,9 +91,13 @@ def tile_attend_gatehop_kernel(tc, notes_words, notes_scales, wb_words, wb_scale
                     start=True, stop=True)
 
         h = [sb.tile([P, U], F32, name="h%d" % t) for t in range(PACK)]
-        s = [sb.tile([P, I], F32, name="s%d" % t) for t in range(PACK)]
+        s = [sb.tile([P, I], F32, name="s%d" % t, tag="slots%d" % t) for t in range(PACK)]
         c = [sb.tile([P, U], F32, name="c%d" % t) for t in range(PACK)]
-        g = [sb.tile([P, PACK, HALF], F32, name="g%d" % a) for a in range(2)]
+        g = {0: sb.tile([P, PACK, CHUNKS[0][1]], F32, name="g0")}
+
+        def picks(a):
+            i0, n = CHUNKS[a]
+            return list3[:, i0 // 16 : (i0 + n) // 16]
 
         def copy_v(t, b):
             nc.vector.tensor_copy(out=h[t][:, BANK * b : BANK * (b + 1)], in_=banks[t][b][:])
@@ -107,10 +112,9 @@ def tile_attend_gatehop_kernel(tc, notes_words, notes_scales, wb_words, wb_scale
         def scatter_v(t):
             nc.vector.tensor_copy(out=f[t][:].indirect(list2[:]), in_=s[t][:])
 
-        def scatter_s(t):
-            for a in range(2):
-                nc.scalar.activation(out=f[t][:].indirect(list2[:, COLS * a : COLS * (a + 1)]),
-                                     in_=s[t][:, HALF * a : HALF * (a + 1)], func=ACT.Copy)
+        def scatter_s(t, a):
+            nc.scalar.activation(out=f[t][:].indirect(list2[:, COLS * a : COLS * (a + 1)]),
+                                 in_=s[t][:, HALF * a : HALF * (a + 1)], func=ACT.Copy)
 
         def add(t):
             for b in range(2):
@@ -119,50 +123,58 @@ def tile_attend_gatehop_kernel(tc, notes_words, notes_scales, wb_words, wb_scale
                                                op0=ALU.mult, op1=ALU.add)
 
         def gather_v(t, a):
-            nc.vector.tensor_copy(out=g[a][:, t, :], in_=c[t][:].indirect(list3[:, COLS * a : COLS * (a + 1)]))
+            nc.vector.tensor_copy(out=g[a][:, t, :], in_=c[t][:].indirect(picks(a)))
 
         def gather_s(t, a):
-            nc.scalar.activation(out=g[a][:, t, :], in_=c[t][:].indirect(list3[:, COLS * a : COLS * (a + 1)]), func=ACT.Copy)
+            nc.scalar.activation(out=g[a][:, t, :], in_=c[t][:].indirect(picks(a)), func=ACT.Copy)
 
         copy_v(0, 0)
-        copy_s(0, 1)
+        copy_v(0, 1)
         sigmoid(0)
         copy_v(1, 0)
         copy_v(1, 1)
-        sigmoid(1)
         copy_v(2, 0)
         copy_v(2, 1)
         scatter_v(0)
-        sigmoid(2)
+        sigmoid(1)
         copy_s(3, 0)
         copy_s(3, 1)
+        sigmoid(2)
         sigmoid(3)
-        scatter_s(2)
         scatter_v(1)
-        scatter_s(3)
+        scatter_s(2, 0)
+        scatter_s(3, 0)
+        scatter_s(2, 1)
+        scatter_s(3, 1)
         add(0)
         add(1)
-        add(2)
         gather_v(0, 0)
-        gather_v(0, 1)
+        add(2)
         add(3)
         gather_s(1, 0)
         gather_s(2, 0)
         gather_v(3, 0)
-        gather_s(1, 1)
-        gather_s(2, 1)
-        gather_s(3, 1)
+        for a in (1, 2):
+            g[a] = sb.tile([P, PACK, CHUNKS[a][1]], F32, name="g%d" % a, tag="slots%d" % (a + 1))
+            for t in range(PACK):
+                gather_s(t, a)
 
-        kf_view = kf4[:].unsqueeze(1).unsqueeze(3).to_broadcast([P, HALF // 4, PACK, 4])
-        for a in range(2):
-            w = sb.tile([P, HALF, PACK], BF16, name="w%d" % a, align_bytes=64)
-            nc.vector.tensor_tensor(out=w[:].rearrange("p (c i) t -> p c t i", i=4),
-                                    in0=g[a][:].rearrange("p t (c i) -> p c t i", i=4), in1=kf_view, op=ALU.mult)
-            wq = sb.tile([P, HALF], U32, name="wq%d" % a, align_bytes=64)
-            wq_plane = sb.tile([P, HALF], U8, name="wq_plane%d" % a, align_bytes=64)
-            nc.vector.quantize_mx(out=wq[:].bitcast(FP8X4), scales=wq_plane[:], in_=w[:].rearrange("p i t -> p (i t)"))
+        kf_view = kf4[:].unsqueeze(1).unsqueeze(3)
+        w = [sb.tile([P, n, PACK], BF16, name="w%d" % a, align_bytes=64) for a, (i0, n) in enumerate(CHUNKS)]
+
+        def weigh(a):
+            n = CHUNKS[a][1]
+            nc.vector.tensor_tensor(out=w[a][:].rearrange("p (c i) t -> p c t i", i=4),
+                                    in0=g[a][:].rearrange("p t (c i) -> p c t i", i=4),
+                                    in1=kf_view.to_broadcast([P, n // 4, PACK, 4]), op=ALU.mult)
+
+        def finish(a):
+            i0, n = CHUNKS[a]
+            wq = sb.tile([P, n], U32, name="wq%d" % a, align_bytes=64)
+            wq_plane = sb.tile([P, n], U8, name="wq_plane%d" % a, align_bytes=64)
+            nc.vector.quantize_mx(out=wq[:].bitcast(FP8X4), scales=wq_plane[:], in_=w[a][:].rearrange("p i t -> p (i t)"))
             for e in range(2):
-                y_ps = ps.tile([P, HALF], F32, name="y_ps%d_%d" % (a, e), tag="bank%d" % (2 * a + e))
+                y_ps = ps.tile([P, n], F32, name="y_ps%d_%d" % (a, e), tag="bank%d" % (2 * a + e))
                 nc.tensor.matmul_mx(
                     out=y_ps[:],
                     lhsT=wo[:, P * e : P * (e + 1)].bitcast(FP8X4),
@@ -170,9 +182,16 @@ def tile_attend_gatehop_kernel(tc, notes_words, notes_scales, wb_words, wb_scale
                     rhs=wq[:].bitcast(FP8X4),
                     rhs_scale=wq_plane[:],
                     start=True, stop=True)
-                y = sb.tile([P, HALF], F32, name="y%d_%d" % (a, e))
-                if a == 1 and e == 1:
+                y = sb.tile([P, n], F32, name="y%d_%d" % (a, e))
+                if a == 2 and e == 0:
                     nc.vector.tensor_copy(out=y[:], in_=y_ps[:])
                 else:
                     nc.scalar.copy(out=y[:], in_=y_ps[:])
-                nc.sync.dma_start(out=out[P * e : P * (e + 1), HALF * a : HALF * (a + 1)], in_=y[:])
+                nc.sync.dma_start(out=out[P * e : P * (e + 1), i0 : i0 + n], in_=y[:])
+
+        weigh(0)
+        weigh(1)
+        finish(0)
+        weigh(2)
+        finish(1)
+        finish(2)

@@ -19,8 +19,9 @@ ACT = mybir.ActivationFunctionType
 P = 128
 PACK = 4
 BANK = 512
+PER_COLUMN = 16
+RUN = 4
 HALF = I // 2
-COLS = HALF // 16
 CHUNKS = [(0, 256), (256, 128), (384, 128)]
 
 
@@ -31,167 +32,163 @@ def tile_attend_gatehop_kernel(tc, notes_words, notes_scales, wb_words, wb_scale
         sb = ctx.enter_context(tc.tile_pool(name="sb", bufs=1))
         ps = ctx.enter_context(tc.psum_pool(name="ps", bufs=1))
 
-        def load_scale_rows(plane, rows, quadrants):
+        def load_scale_rows(scale_tile, rows, quadrants):
             for q in quadrants:
-                nc.sync.dma_start(out=plane[32 * q : 32 * q + 4, :].bitcast(I32), in_=rows[0, 4 * q : 4 * q + 4, :].bitcast(I32))
+                nc.sync.dma_start(out=scale_tile[32 * q : 32 * q + 4, :].bitcast(I32),
+                                  in_=rows[0, 4 * q : 4 * q + 4, :].bitcast(I32))
 
-        wb_plane_raw = sb.tile([P, K], U8, name="wb_plane_raw", tag="raw_plane_then_f2", align_bytes=64)
-        notes_plane = sb.tile([P, U], U8, name="notes_plane", align_bytes=64)
-        wo_plane = sb.tile([P, E], U8, name="wo_plane", align_bytes=64)
-        nc.gpsimd.memset(wb_plane_raw[:].bitcast(U32), 0)
+        wb_raw = sb.tile([P, 3 * K], U8, name="wb_raw", tag="wb_raw_then_f3", align_bytes=64)
+        wb_raw_words = wb_raw[:, 0 : 2 * K]
+        wb_raw_scales = wb_raw[:, 2 * K : 3 * K]
+        notes_sc = sb.tile([P, U], U8, name="notes_sc", align_bytes=64)
+        wo_sc = sb.tile([P, E], U8, name="wo_sc", align_bytes=64)
+        nc.gpsimd.memset(wb_raw_scales.bitcast(U32), 0)
 
-        wb_raw = sb.tile([P, 2 * K], U8, name="wb_raw", tag="raw_words_then_f3", align_bytes=64)
-        load_scale_rows(notes_plane, notes_scales, range(2))
-        load_scale_rows(wb_plane_raw, wb_scales, range(4))
-        nc.sync.dma_start(out=wb_raw[:].bitcast(I32), in_=wb_words[0].bitcast(I32))
+        load_scale_rows(notes_sc, notes_scales, range(2))
+        load_scale_rows(wb_raw_scales, wb_scales, range(4))
+        nc.sync.dma_start(out=wb_raw_words.bitcast(I32), in_=wb_words[0].bitcast(I32))
         notes = sb.tile([P, U], U32, name="notes", align_bytes=64)
         nc.sync.dma_start(out=notes[:].bitcast(I32), in_=notes_words[0].rearrange("p n t -> p (n t)").bitcast(I32))
-        load_scale_rows(notes_plane, notes_scales, range(2, 4))
+        load_scale_rows(notes_sc, notes_scales, range(2, 4))
 
-        list1 = sb.tile([P, I // 16], U16, name="list1")
-        list2 = sb.tile([P, I // 16], U16, name="list2")
-        list3 = sb.tile([P, I // 16], U16, name="list3")
+        idx = sb.tile([P, I // PER_COLUMN], U16, name="idx")
+        idx2 = sb.tile([P, I // PER_COLUMN], U16, name="idx2")
+        idx3 = sb.tile([P, I // PER_COLUMN], U16, name="idx3")
         slope4 = sb.tile([P, PACK], F32, name="slope4")
         bias4 = sb.tile([P, PACK], F32, name="bias4")
         kf4 = sb.tile([P, PACK], F32, name="kf4")
-        nc.sync.dma_start(list1[:], offs)
+        nc.sync.dma_start(idx[:], offs)
         nc.sync.dma_start(out=slope4[:], in_=slope.rearrange("(p t) o -> p (t o)", t=PACK))
         nc.sync.dma_start(out=bias4[:], in_=bias.rearrange("(p t) o -> p (t o)", t=PACK))
-        nc.sync.dma_start(list2[:], offs2)
-        nc.sync.dma_start(list3[:], offs3)
+        nc.sync.dma_start(idx2[:], offs2)
+        nc.sync.dma_start(idx3[:], offs3)
         nc.sync.dma_start(out=kf4[:], in_=kf.rearrange("(p t) o -> p (t o)", t=PACK))
         wo = sb.tile([P, E], U32, name="wo", align_bytes=64)
         nc.sync.dma_start(out=wo[:].bitcast(I32), in_=wo_words[0].rearrange("p n t -> p (n t)").bitcast(I32))
-        load_scale_rows(wo_plane, wo_scales, range(4))
+        load_scale_rows(wo_sc, wo_scales, range(4))
 
-        f = [sb.tile([P, U], F32, name="f%d" % t) for t in range(2)]
-        for t in range(2):
-            nc.vector.memset(f[t][:], 0.0)
+        f = [sb.tile([P, U], F32, name="f%d" % t) for t in range(PACK - 1)]
+        for t in range(PACK - 1):
+            nc.vector.memset(f[t][:].bitcast(I32), 0)
 
         wb = sb.tile([P, 2 * K], U8, name="wb", align_bytes=64)
-        wb_plane = sb.tile([P, K], U8, name="wb_plane", align_bytes=64)
+        wb_sc = sb.tile([P, K], U8, name="wb_sc", align_bytes=64)
         nc.vector.tensor_copy(out=wb[:].bitcast(U16).rearrange("p (t m) -> p t m", t=PACK),
-                       in_=wb_raw[:].bitcast(U16).rearrange("p (m t) -> p t m", t=PACK))
-        nc.vector.tensor_copy(out=wb_plane[:].rearrange("p (t m) -> p t m", t=PACK),
-                              in_=wb_plane_raw[:].rearrange("p (m t) -> p t m", t=PACK))
-        f.append(sb.tile([P, U], F32, name="f2", tag="raw_plane_then_f2", align_bytes=64))
-        f.append(sb.tile([P, U], F32, name="f3", tag="raw_words_then_f3", align_bytes=64))
-        nc.gpsimd.memset(f[3][:], 0.0)
-        nc.gpsimd.memset(f[2][:], 0.0)
+                              in_=wb_raw_words.bitcast(U16).rearrange("p (m t) -> p t m", t=PACK))
+        nc.vector.tensor_copy(out=wb_sc[:].rearrange("p (t m) -> p t m", t=PACK),
+                              in_=wb_raw_scales.rearrange("p (m t) -> p t m", t=PACK))
+        f.append(sb.tile([P, U], F32, name="f3", tag="wb_raw_then_f3", align_bytes=64))
+        nc.gpsimd.memset(f[3][:].bitcast(I32), 0)
 
-        banks = [[ps.tile([P, BANK], F32, name="h_ps%d_%d" % (t, b), tag="bank%d" % (2 * t + b)) for b in range(2)] for t in range(PACK)]
+        h_ps = [[ps.tile([P, BANK], F32, name="h_ps%d_%d" % (t, b), tag="bank%d" % (2 * t + b)) for b in range(2)]
+                for t in range(PACK)]
         for t in range(PACK):
             for b in range(2):
                 nc.tensor.matmul_mx(
-                    out=banks[t][b][:],
+                    out=h_ps[t][b][:],
                     lhsT=wb[:, 2 * P * t : 2 * P * (t + 1)].bitcast(FP4X4),
-                    lhsT_scale=wb_plane[:, P * t : P * (t + 1)],
+                    lhsT_scale=wb_sc[:, P * t : P * (t + 1)],
                     rhs=notes[:, BANK * b : BANK * (b + 1)].bitcast(FP8X4),
-                    rhs_scale=notes_plane[:, BANK * b : BANK * (b + 1)],
+                    rhs_scale=notes_sc[:, BANK * b : BANK * (b + 1)],
                     start=True, stop=True)
 
-        h = [sb.tile([P, U], F32, name="h%d" % t) for t in range(PACK)]
+        h = [sb.tile([P, U], F32, name="h%d" % t, tag="row%d" % t) for t in range(PACK)]
         s = [sb.tile([P, I], F32, name="s%d" % t, tag="slots%d" % t) for t in range(PACK)]
-        c = [sb.tile([P, U], F32, name="c%d" % t) for t in range(PACK)]
-        g = {0: sb.tile([P, PACK, CHUNKS[0][1]], F32, name="g0")}
+        c = [sb.tile([P, U], F32, name="c%d" % t) for t in range(2)]
 
-        def picks(a):
-            i0, n = CHUNKS[a]
-            return list3[:, i0 // 16 : (i0 + n) // 16]
+        def entries(offsets, i0, n):
+            return offsets[:, i0 // PER_COLUMN : (i0 + n) // PER_COLUMN]
 
-        def copy_v(t, b):
-            nc.vector.tensor_copy(out=h[t][:, BANK * b : BANK * (b + 1)], in_=banks[t][b][:])
+        def bank_cols(b):
+            return slice(BANK * b, BANK * (b + 1))
 
-        def copy_s(t, b):
-            nc.scalar.copy(out=h[t][:, BANK * b : BANK * (b + 1)], in_=banks[t][b][:])
+        def to_sbuf(copy, t):
+            for b in range(2):
+                copy(out=h[t][:, bank_cols(b)], in_=h_ps[t][b][:])
 
         def sigmoid(t):
-            nc.scalar.activation(out=s[t][:], in_=h[t][:].indirect(list1[:]), func=ACT.Sigmoid,
+            nc.scalar.activation(out=s[t][:], in_=h[t][:].indirect(idx[:]), func=ACT.Sigmoid,
                                  bias=bias4[:, t : t + 1], scale=slope4[:, t : t + 1])
 
-        def scatter_v(t):
-            nc.vector.tensor_copy(out=f[t][:].indirect(list2[:]), in_=s[t][:])
+        def scatter_on_vector(t, i0, n):
+            nc.vector.tensor_copy(out=f[t][:].indirect(entries(idx2, i0, n)), in_=s[t][:, i0 : i0 + n])
 
-        def scatter_s(t, a):
-            nc.scalar.activation(out=f[t][:].indirect(list2[:, COLS * a : COLS * (a + 1)]),
-                                 in_=s[t][:, HALF * a : HALF * (a + 1)], func=ACT.Copy)
+        def scatter_on_scalar(t, i0, n):
+            nc.scalar.activation(out=f[t][:].indirect(entries(idx2, i0, n)), in_=s[t][:, i0 : i0 + n], func=ACT.Copy)
 
-        def add(t):
-            for b in range(2):
-                cols = slice(BANK * b, BANK * (b + 1))
-                nc.vector.scalar_tensor_tensor(out=c[t][:, cols], in0=f[t][:, cols], scalar=2.0, in1=banks[t][b][:],
-                                               op0=ALU.mult, op1=ALU.add)
+        def sum_on_gpsimd(t, cols):
+            twice = sb.tile([P, cols.stop - cols.start], F32, name="twice%d" % t, tag="twice")
+            nc.gpsimd.tensor_scalar(out=twice[:], in0=f[t][:, cols], scalar1=2.0, scalar2=0.0, op0=ALU.mult, op1=ALU.add)
+            nc.gpsimd.tensor_tensor(out=c[t][:, cols], in0=h[t][:, cols], in1=twice[:], op=ALU.add)
 
-        def gather_v(t, a):
-            nc.vector.tensor_copy(out=g[a][:, t, :], in_=c[t][:].indirect(picks(a)))
+        def sum_on_vector(t, b):
+            nc.vector.scalar_tensor_tensor(out=c[t][:, bank_cols(b)], in0=f[t][:, bank_cols(b)], scalar=2.0,
+                                           in1=h_ps[t][b][:], op0=ALU.mult, op1=ALU.add)
 
-        def gather_s(t, a):
-            nc.scalar.activation(out=g[a][:, t, :], in_=c[t][:].indirect(picks(a)), func=ACT.Copy)
-
-        copy_v(0, 0)
-        copy_v(0, 1)
+        to_sbuf(nc.vector.tensor_copy, 0)
         sigmoid(0)
-        copy_v(1, 0)
-        copy_v(1, 1)
-        copy_v(2, 0)
-        copy_v(2, 1)
-        scatter_v(0)
+        to_sbuf(nc.vector.tensor_copy, 1)
+        to_sbuf(nc.vector.tensor_copy, 2)
+        scatter_on_vector(0, 0, I)
         sigmoid(1)
-        copy_s(3, 0)
-        copy_s(3, 1)
+        to_sbuf(nc.scalar.copy, 3)
         sigmoid(2)
         sigmoid(3)
-        scatter_v(1)
-        scatter_s(2, 0)
-        scatter_s(3, 0)
-        scatter_s(2, 1)
-        scatter_s(3, 1)
-        add(0)
-        add(1)
-        gather_v(0, 0)
-        add(2)
-        add(3)
-        gather_s(1, 0)
-        gather_s(2, 0)
-        gather_v(3, 0)
-        for a in (1, 2):
-            g[a] = sb.tile([P, PACK, CHUNKS[a][1]], F32, name="g%d" % a, tag="slots%d" % (a + 1))
-            for t in range(PACK):
-                gather_s(t, a)
+        scatter_on_vector(1, 0, I)
+        sum_on_gpsimd(0, slice(0, U))
+        scatter_on_scalar(2, 0, HALF)
+        scatter_on_scalar(3, 0, HALF)
+        scatter_on_vector(2, HALF, HALF)
+        scatter_on_scalar(3, HALF, HALF)
+        sum_on_gpsimd(1, bank_cols(0))
+        sum_on_vector(1, 1)
+        for t in (2, 3):
+            c.append(sb.tile([P, U], F32, name="c%d" % t, tag="row%d" % (t - 2)))
+            for b in range(2):
+                sum_on_vector(t, b)
 
-        kf_view = kf4[:].unsqueeze(1).unsqueeze(3)
+        picked_all = sb.tile([P, PACK * I], F32, name="picked_all", tag="slots3")
+        picked = [picked_all[:, PACK * i0 : PACK * (i0 + n)].rearrange("p (t i) -> p t i", t=PACK) for i0, n in CHUNKS]
+        for a, (i0, n) in enumerate(CHUNKS):
+            for t in range(PACK):
+                looked_up = c[t][:].indirect(entries(idx3, i0, n))
+                if a == 0 and t == PACK - 1:
+                    nc.vector.tensor_copy(out=picked[a][:, t, :], in_=looked_up)
+                else:
+                    nc.scalar.activation(out=picked[a][:, t, :], in_=looked_up, func=ACT.Copy)
+
         w = [sb.tile([P, n, PACK], BF16, name="w%d" % a, align_bytes=64) for a, (i0, n) in enumerate(CHUNKS)]
 
         def weigh(a):
             n = CHUNKS[a][1]
-            nc.vector.tensor_tensor(out=w[a][:].rearrange("p (c i) t -> p c t i", i=4),
-                                    in0=g[a][:].rearrange("p t (c i) -> p c t i", i=4),
-                                    in1=kf_view.to_broadcast([P, n // 4, PACK, 4]), op=ALU.mult)
+            nc.vector.tensor_tensor(out=w[a][:].rearrange("p (r i) t -> p r t i", i=RUN),
+                                    in0=picked[a].rearrange("p t (r i) -> p r t i", i=RUN),
+                                    in1=kf4[:].unsqueeze(1).unsqueeze(3).to_broadcast([P, n // RUN, PACK, RUN]),
+                                    op=ALU.mult)
 
         def finish(a):
             i0, n = CHUNKS[a]
             wq = sb.tile([P, n], U32, name="wq%d" % a, align_bytes=64)
-            wq_plane = sb.tile([P, n], U8, name="wq_plane%d" % a, align_bytes=64)
-            nc.vector.quantize_mx(out=wq[:].bitcast(FP8X4), scales=wq_plane[:], in_=w[a][:].rearrange("p i t -> p (i t)"))
-            for e in range(2):
+            wq_sc = sb.tile([P, n], U8, name="wq_sc%d" % a, align_bytes=64)
+            nc.vector.quantize_mx(out=wq[:].bitcast(FP8X4), scales=wq_sc[:], in_=w[a][:].rearrange("p i t -> p (i t)"))
+            for e in range(E // P):
                 y_ps = ps.tile([P, n], F32, name="y_ps%d_%d" % (a, e), tag="bank%d" % (2 * a + e))
                 nc.tensor.matmul_mx(
                     out=y_ps[:],
                     lhsT=wo[:, P * e : P * (e + 1)].bitcast(FP8X4),
-                    lhsT_scale=wo_plane[:, P * e : P * (e + 1)],
+                    lhsT_scale=wo_sc[:, P * e : P * (e + 1)],
                     rhs=wq[:].bitcast(FP8X4),
-                    rhs_scale=wq_plane[:],
+                    rhs_scale=wq_sc[:],
                     start=True, stop=True)
                 y = sb.tile([P, n], F32, name="y%d_%d" % (a, e))
-                if a == 2 and e == 0:
+                if a == len(CHUNKS) - 1 and e == 0:
                     nc.vector.tensor_copy(out=y[:], in_=y_ps[:])
                 else:
                     nc.scalar.copy(out=y[:], in_=y_ps[:])
                 nc.sync.dma_start(out=out[P * e : P * (e + 1), i0 : i0 + n], in_=y[:])
 
         weigh(0)
-        weigh(1)
-        finish(0)
-        weigh(2)
-        finish(1)
-        finish(2)
+        for a in range(len(CHUNKS)):
+            if a + 1 < len(CHUNKS):
+                weigh(a + 1)
+            finish(a)

from contextlib import ExitStack

import concourse.mybir as mybir

D, K, U, I, E = 512, 512, 1024, 512, 256
FLOPS = 2 * D * K * U + 2 * K * E * I

F32 = mybir.dt.float32
BF16 = mybir.dt.bfloat16
I32 = mybir.dt.int32
U32 = mybir.dt.uint32
U16 = mybir.dt.uint16
U8 = mybir.dt.uint8
FP8X4 = mybir.dt.float8_e4m3fn_x4
FP4X4 = mybir.dt.float4_e2m1fn_x4
ALU = mybir.AluOpType
ACT = mybir.ActivationFunctionType

P = 128
PACK = 4
BANK = 512
PER_COLUMN = 16
RUN = 4
HALF = I // 2
CHUNKS = [(0, 256), (256, 128), (384, 128)]


def tile_attend_gatehop_kernel(tc, notes_words, notes_scales, wb_words, wb_scales, bias, slope, kf,
                                wo_words, wo_scales, offs, offs2, offs3, out):
    nc = tc.nc
    with ExitStack() as ctx:
        sb = ctx.enter_context(tc.tile_pool(name="sb", bufs=1))
        ps = ctx.enter_context(tc.psum_pool(name="ps", bufs=1))

        def load_scale_rows(scale_tile, rows, quadrants):
            for q in quadrants:
                nc.sync.dma_start(out=scale_tile[32 * q : 32 * q + 4, :].bitcast(I32),
                                  in_=rows[0, 4 * q : 4 * q + 4, :].bitcast(I32))

        wb_raw = sb.tile([P, 3 * K], U8, name="wb_raw", tag="wb_raw_then_f3", align_bytes=64)
        wb_raw_words = wb_raw[:, 0 : 2 * K]
        wb_raw_scales = wb_raw[:, 2 * K : 3 * K]
        notes_sc = sb.tile([P, U], U8, name="notes_sc", align_bytes=64)
        wo_sc = sb.tile([P, E], U8, name="wo_sc", align_bytes=64)
        nc.gpsimd.memset(wb_raw_scales.bitcast(U32), 0)

        load_scale_rows(notes_sc, notes_scales, range(2))
        load_scale_rows(wb_raw_scales, wb_scales, range(4))
        nc.sync.dma_start(out=wb_raw_words.bitcast(I32), in_=wb_words[0].bitcast(I32))
        notes = sb.tile([P, U], U32, name="notes", align_bytes=64)
        nc.sync.dma_start(out=notes[:].bitcast(I32), in_=notes_words[0].rearrange("p n t -> p (n t)").bitcast(I32))
        load_scale_rows(notes_sc, notes_scales, range(2, 4))

        idx = sb.tile([P, I // PER_COLUMN], U16, name="idx")
        idx2 = sb.tile([P, I // PER_COLUMN], U16, name="idx2")
        idx3 = sb.tile([P, I // PER_COLUMN], U16, name="idx3")
        slope4 = sb.tile([P, PACK], F32, name="slope4")
        bias4 = sb.tile([P, PACK], F32, name="bias4")
        kf4 = sb.tile([P, PACK], F32, name="kf4")
        nc.sync.dma_start(idx[:], offs)
        nc.sync.dma_start(out=slope4[:], in_=slope.rearrange("(p t) o -> p (t o)", t=PACK))
        nc.sync.dma_start(out=bias4[:], in_=bias.rearrange("(p t) o -> p (t o)", t=PACK))
        nc.sync.dma_start(idx2[:], offs2)
        nc.sync.dma_start(idx3[:], offs3)
        nc.sync.dma_start(out=kf4[:], in_=kf.rearrange("(p t) o -> p (t o)", t=PACK))
        wo = sb.tile([P, E], U32, name="wo", align_bytes=64)
        nc.sync.dma_start(out=wo[:].bitcast(I32), in_=wo_words[0].rearrange("p n t -> p (n t)").bitcast(I32))
        load_scale_rows(wo_sc, wo_scales, range(4))

        f = [sb.tile([P, U], F32, name="f%d" % t) for t in range(PACK - 1)]
        for t in range(PACK - 1):
            nc.vector.memset(f[t][:].bitcast(I32), 0)

        wb = sb.tile([P, 2 * K], U8, name="wb", align_bytes=64)
        wb_sc = sb.tile([P, K], U8, name="wb_sc", align_bytes=64)
        nc.vector.tensor_copy(out=wb[:].bitcast(U16).rearrange("p (t m) -> p t m", t=PACK),
                              in_=wb_raw_words.bitcast(U16).rearrange("p (m t) -> p t m", t=PACK))
        nc.vector.tensor_copy(out=wb_sc[:].rearrange("p (t m) -> p t m", t=PACK),
                              in_=wb_raw_scales.rearrange("p (m t) -> p t m", t=PACK))
        f.append(sb.tile([P, U], F32, name="f3", tag="wb_raw_then_f3", align_bytes=64))
        nc.gpsimd.memset(f[3][:].bitcast(I32), 0)

        h_ps = [[ps.tile([P, BANK], F32, name="h_ps%d_%d" % (t, b), tag="bank%d" % (2 * t + b)) for b in range(2)]
                for t in range(PACK)]
        for t in range(PACK):
            for b in range(2):
                nc.tensor.matmul_mx(
                    out=h_ps[t][b][:],
                    lhsT=wb[:, 2 * P * t : 2 * P * (t + 1)].bitcast(FP4X4),
                    lhsT_scale=wb_sc[:, P * t : P * (t + 1)],
                    rhs=notes[:, BANK * b : BANK * (b + 1)].bitcast(FP8X4),
                    rhs_scale=notes_sc[:, BANK * b : BANK * (b + 1)],
                    start=True, stop=True)

        h = [sb.tile([P, U], F32, name="h%d" % t, tag="row%d" % t) for t in range(PACK)]
        s = [sb.tile([P, I], F32, name="s%d" % t, tag="slots%d" % t) for t in range(PACK)]
        c = [sb.tile([P, U], F32, name="c%d" % t) for t in range(2)]

        def entries(offsets, i0, n):
            return offsets[:, i0 // PER_COLUMN : (i0 + n) // PER_COLUMN]

        def bank_cols(b):
            return slice(BANK * b, BANK * (b + 1))

        def to_sbuf(copy, t):
            for b in range(2):
                copy(out=h[t][:, bank_cols(b)], in_=h_ps[t][b][:])

        def sigmoid(t):
            nc.scalar.activation(out=s[t][:], in_=h[t][:].indirect(idx[:]), func=ACT.Sigmoid,
                                 bias=bias4[:, t : t + 1], scale=slope4[:, t : t + 1])

        def scatter_on_vector(t, i0, n):
            nc.vector.tensor_copy(out=f[t][:].indirect(entries(idx2, i0, n)), in_=s[t][:, i0 : i0 + n])

        def scatter_on_scalar(t, i0, n):
            nc.scalar.activation(out=f[t][:].indirect(entries(idx2, i0, n)), in_=s[t][:, i0 : i0 + n], func=ACT.Copy)

        def sum_on_gpsimd(t, cols):
            twice = sb.tile([P, cols.stop - cols.start], F32, name="twice%d" % t, tag="twice")
            nc.gpsimd.tensor_scalar(out=twice[:], in0=f[t][:, cols], scalar1=2.0, scalar2=0.0, op0=ALU.mult, op1=ALU.add)
            nc.gpsimd.tensor_tensor(out=c[t][:, cols], in0=h[t][:, cols], in1=twice[:], op=ALU.add)

        def sum_on_vector(t, b):
            nc.vector.scalar_tensor_tensor(out=c[t][:, bank_cols(b)], in0=f[t][:, bank_cols(b)], scalar=2.0,
                                           in1=h_ps[t][b][:], op0=ALU.mult, op1=ALU.add)

        to_sbuf(nc.vector.tensor_copy, 0)
        sigmoid(0)
        to_sbuf(nc.vector.tensor_copy, 1)
        to_sbuf(nc.vector.tensor_copy, 2)
        scatter_on_vector(0, 0, I)
        sigmoid(1)
        to_sbuf(nc.scalar.copy, 3)
        sigmoid(2)
        sigmoid(3)
        scatter_on_vector(1, 0, I)
        sum_on_gpsimd(0, slice(0, U))
        scatter_on_scalar(2, 0, HALF)
        scatter_on_scalar(3, 0, HALF)
        scatter_on_vector(2, HALF, HALF)
        scatter_on_scalar(3, HALF, HALF)
        sum_on_gpsimd(1, bank_cols(0))
        sum_on_vector(1, 1)
        for t in (2, 3):
            c.append(sb.tile([P, U], F32, name="c%d" % t, tag="row%d" % (t - 2)))
            for b in range(2):
                sum_on_vector(t, b)

        picked_all = sb.tile([P, PACK * I], F32, name="picked_all", tag="slots3")
        picked = [picked_all[:, PACK * i0 : PACK * (i0 + n)].rearrange("p (t i) -> p t i", t=PACK) for i0, n in CHUNKS]
        for a, (i0, n) in enumerate(CHUNKS):
            for t in range(PACK):
                looked_up = c[t][:].indirect(entries(idx3, i0, n))
                if a == 0 and t == PACK - 1:
                    nc.vector.tensor_copy(out=picked[a][:, t, :], in_=looked_up)
                else:
                    nc.scalar.activation(out=picked[a][:, t, :], in_=looked_up, func=ACT.Copy)

        w = [sb.tile([P, n, PACK], BF16, name="w%d" % a, align_bytes=64) for a, (i0, n) in enumerate(CHUNKS)]

        def weigh(a):
            n = CHUNKS[a][1]
            nc.vector.tensor_tensor(out=w[a][:].rearrange("p (r i) t -> p r t i", i=RUN),
                                    in0=picked[a].rearrange("p t (r i) -> p r t i", i=RUN),
                                    in1=kf4[:].unsqueeze(1).unsqueeze(3).to_broadcast([P, n // RUN, PACK, RUN]),
                                    op=ALU.mult)

        def finish(a):
            i0, n = CHUNKS[a]
            wq = sb.tile([P, n], U32, name="wq%d" % a, align_bytes=64)
            wq_sc = sb.tile([P, n], U8, name="wq_sc%d" % a, align_bytes=64)
            nc.vector.quantize_mx(out=wq[:].bitcast(FP8X4), scales=wq_sc[:], in_=w[a][:].rearrange("p i t -> p (i t)"))
            for e in range(E // P):
                y_ps = ps.tile([P, n], F32, name="y_ps%d_%d" % (a, e), tag="bank%d" % (2 * a + e))
                nc.tensor.matmul_mx(
                    out=y_ps[:],
                    lhsT=wo[:, P * e : P * (e + 1)].bitcast(FP8X4),
                    lhsT_scale=wo_sc[:, P * e : P * (e + 1)],
                    rhs=wq[:].bitcast(FP8X4),
                    rhs_scale=wq_sc[:],
                    start=True, stop=True)
                y = sb.tile([P, n], F32, name="y%d_%d" % (a, e))
                if a == len(CHUNKS) - 1 and e == 0:
                    nc.vector.tensor_copy(out=y[:], in_=y_ps[:])
                else:
                    nc.scalar.copy(out=y[:], in_=y_ps[:])
                nc.sync.dma_start(out=out[P * e : P * (e + 1), i0 : i0 + n], in_=y[:])

        weigh(0)
        for a in range(len(CHUNKS)):
            if a + 1 < len(CHUNKS):
                weigh(a + 1)
            finish(a)
